import numpy as np
import ml_dtypes


def mxq(x, axis, fmt="e4m3"):
    dtype, down = {"e4m3": (ml_dtypes.float8_e4m3fn, 7), "e5m2": (ml_dtypes.float8_e5m2, 14)}[fmt]
    v = np.moveaxis(np.asarray(x, np.float32).astype(ml_dtypes.bfloat16).astype(np.float64), axis, -1)
    blocks = v.reshape(v.shape[:-1] + (-1, 32))
    amax = np.abs(blocks).max(-1, keepdims=True)
    byte = np.maximum(np.where(amax > 0, np.frexp(amax)[1] - 1 + 127, 0) - down, 1)
    scale = np.exp2(byte - 127.0)
    codes = (blocks / scale).astype(np.float32).astype(dtype).astype(np.float64)
    return np.moveaxis((codes * scale).reshape(v.shape), -1, axis)


WIDE = False


def mx_kscale(k):
    if not WIDE:
        return np.ones(k)
    levels = np.array([10, -10, 5, -5, 0])
    if k % 512:
        return np.exp2(np.random.permutation(np.resize(levels, k // 32))).repeat(32)
    a = np.empty((k // 512, 16))
    for p in range(k // 512):
        a[p, :8] = np.random.permutation(np.resize(levels, 8))
        for g in range(8):
            far = levels[np.abs(levels - a[p, g]) >= 10]
            a[p, g + 8] = far[np.random.randint(len(far))]
    return np.exp2(a.ravel()).repeat(32)


BF16 = ml_dtypes.bfloat16


def bf(x):
    return np.asarray(x, np.float32).astype(BF16)


def f64(x):
    return np.asarray(x).astype(np.float64)


B, N, R, W = 4, 512, 256, 512


def update_link(link, w, p):
    w_row = w[:, :, None]
    w_col = w[:, None, :]
    l2 = (1.0 - w_row - w_col) * link + w_row * p[:, None, :]
    idx = np.arange(link.shape[-1])
    on_diag = idx[:, None] == idx[None, :]
    return np.where(on_diag[None, :, :], 0.0, l2)


def draw0():
    s, t = mx_kscale(N), mx_kscale(N)
    return {"link": bf(np.random.standard_normal((B, N, N)) / np.sqrt(N)),
            "w": bf(np.random.uniform(0.0, 0.5, (B, N))),
            "p": bf(np.random.standard_normal((B, N)) * 2.25 / np.sqrt(N)),
            "r": bf(np.random.standard_normal((B, R, N)) * s),
            "g": bf((1.0 + 0.1 * np.random.standard_normal(N)) / s),
            "h": bf((1.0 + 0.1 * np.random.standard_normal(N)) * t),
            "m": bf(np.random.standard_normal((B, N, W)) / np.sqrt(N) / t[:, None])}


def core(link, w, p, r, g, h, m):
    l2 = update_link(f64(link), f64(w), f64(p))
    g, h = f64(g), f64(h)
    rq = mxq(f64(r), 2, "e4m3")
    lf = mxq(l2 * g[None, None, :], 2, "e4m3")
    fw = rq @ lf.transpose(0, 2, 1)
    lb = mxq(l2 * g[None, :, None], 1, "e4m3")
    bw = rq @ lb
    a = (0.7 * fw + 0.3 * bw) * h[None, None, :]
    return mxq(a, 2, "e4m3") @ mxq(f64(m), 1, "e4m3")


def e4m3fn_bytes(y):
    return np.clip(np.asarray(y, np.float64), -448.0, 448.0).astype(np.float32).astype(ml_dtypes.float8_e4m3fn).view(np.uint8)


def e4m3fn_values(b):
    return np.asarray(b, np.uint8).view(ml_dtypes.float8_e4m3fn).astype(np.float64)


def setup_inputs():
    d = draw0()
    x0 = np.asarray(d['m']).astype(np.float64)
    s = (np.max(np.abs(x0), axis=(0, 2), keepdims=True) / 448.0).astype(np.float32)
    out = {}
    for k, v in d.items():
        if k == 'm':
            out['m_bytes'] = e4m3fn_bytes(x0 / s.astype(np.float64))
            out['m_scale'] = s
        else:
            out[k] = v
    return out


def reference(link, w, p, r, g, h, m_bytes, m_scale):
    return core(link, w, p, r, g, h, e4m3fn_values(m_bytes) * m_scale.astype(np.float64))

@@ -1,0 +1,380 @@
+from contextlib import ExitStack
+
+import concourse.mybir as mybir
+from concourse.masks import make_identity
+
+B, N, R, W = 4, 512, 256, 512
+FLOPS = 3 * B * 2 * R * N * N
+
+F32 = mybir.dt.float32
+BF16 = mybir.dt.bfloat16
+U32 = mybir.dt.uint32
+U8 = mybir.dt.uint8
+FP8 = mybir.dt.float8_e4m3fn
+FP8X4 = mybir.dt.float8_e4m3fn_x4
+ADD = mybir.AluOpType.add
+SUB = mybir.AluOpType.subtract
+MUL = mybir.AluOpType.mult
+COPY = mybir.ActivationFunctionType.Copy
+
+P = 128
+V_BLOCKS = {3: (0, 1)}
+
+
+def tile_dnctemporallinkreadout_kernel(tc, link, w, p, r, g, h, m_bytes, m_scale, out):
+    nc = tc.nc
+    with ExitStack() as ctx:
+        sb = ctx.enter_context(tc.tile_pool(name="sb", bufs=1))
+        ps = ctx.enter_context(tc.psum_pool(name="ps", bufs=1))
+        ctx.enter_context(tc.manual_schedule())
+
+        rows = sb.tile([P, N], BF16, name="rows")
+        nc.vector.memset(rows[:], 0.0)
+        ident_bf = sb.tile([P, P], BF16, name="ident_bf")
+        make_identity(nc, ident_bf[:])
+        ident = sb.tile([P, P], F32, name="ident")
+        make_identity(nc, ident[:])
+        nc.scalar.dma_start(out=rows[0:4, :], in_=w)
+        nc.scalar.dma_start(out=rows[4:8, :], in_=p)
+        nc.scalar.dma_start(out=rows[8:9, :], in_=g.rearrange("(o n) -> o n", o=1))
+        nc.scalar.dma_start(out=rows[9:10, :], in_=h.rearrange("(o n) -> o n", o=1))
+        ms = sb.tile([P, 4], F32, name="ms")
+        nc.scalar.dma_start(out=ms[:], in_=m_scale.rearrange("o (p t) x -> p (o t x)", t=4))
+
+        lk = {}
+        rr = {}
+        mb = {}
+
+        def load_link(b):
+            lk[b] = sb.tile([P, 4, N], BF16, name=f"lk{b}", align_bytes=64)
+            src = link[b].rearrange("(p t) j -> p t j", t=4)
+            for u in range(2):
+                nc.sync.dma_start(out=lk[b][:, 2 * u : 2 * u + 2, :], in_=src[:, 2 * u : 2 * u + 2, :])
+
+        def load_r(b):
+            rr[b] = sb.tile([P, 2, N], BF16, name=f"rr{b}", align_bytes=64)
+            nc.sync.dma_start(out=rr[b][:], in_=r[b].rearrange("(p a) j -> p a j", a=2))
+
+        def load_m(b):
+            mb[b] = sb.tile([P, 4, W], U8, name=f"mb{b}", align_bytes=64)
+            nc.sync.dma_start(out=mb[b][:], in_=m_bytes[b].rearrange("(p t) w -> p t w", t=4))
+
+        load_link(0)
+        load_r(0)
+        load_m(0)
+        load_link(1)
+        load_m(1)
+        load_r(1)
+        load_link(2)
+        load_m(2)
+        load_r(2)
+        load_link(3)
+        load_m(3)
+        load_r(3)
+
+        not_i = sb.tile([P, P], F32, name="not_i")
+        nc.vector.tensor_scalar(out=not_i[:], in0=ident[:], scalar1=-1.0, scalar2=1.0, op0=MUL, op1=ADD)
+        scp = ps.tile([P, 4, P], BF16, name="scp", tag="tp", bufs=2)
+        for t in range(4):
+            nc.tensor.transpose(scp[:, t, :], rows[:, t : N : 4], ident_bf[:])
+
+        row_ps = {}
+
+        def broadcast_rows(b):
+            row_ps[b] = ps.tile([P, 2 * N], BF16, name=f"row_ps{b}", tag="row", bufs=2)
+            for u in range(2):
+                k = 4 * u + b
+                nc.tensor.matmul(
+                    row_ps[b][:, u * N : (u + 1) * N].rearrange("p (t m) -> p t m", t=4),
+                    lhsT=ident_bf[:, k : k + 1].to_broadcast([P, P]),
+                    rhs=rows[:].rearrange("k (m t) -> k t m", t=4),
+                    start=True,
+                    stop=True,
+                )
+
+        broadcast_rows(0)
+        sc = sb.tile([P, 4, 10], F32, name="sc")
+        nc.vector.tensor_copy(out=sc[:], in_=scp[:, :, 0:10])
+        wm1 = sb.tile([P, 4, 4], F32, name="wm1")
+        nc.vector.tensor_scalar(out=wm1[:], in0=sc[:, :, 0:4], scalar1=-1.0, scalar2=None, op0=ADD)
+        g4 = sb.tile([P, 4], F32, name="g4")
+        nc.scalar.copy(out=g4[:], in_=sc[:, :, 8])
+        h7 = sb.tile([P, 4], F32, name="h7")
+        nc.scalar.activation(out=h7[:], in_=sc[:, :, 9], func=COPY, scale=0.7)
+        h3 = sb.tile([P, 4], F32, name="h3")
+        nc.scalar.activation(out=h3[:], in_=sc[:, :, 9], func=COPY, scale=0.3)
+        gm = sb.tile([P, 4, P, 4], BF16, name="gm", align_bytes=64)
+        for t in range(4):
+            nc.scalar.copy(out=gm[:, t, :, :], in_=g4[:].unsqueeze(1).to_broadcast([P, P, 4]))
+            nc.scalar.activation(out=gm[:, t, :, t], in_=not_i[:], func=COPY, scale=g4[:, t : t + 1])
+
+        xs, l2, tp, lfg, lbg = {}, {}, {}, {}, {}
+        lfc, lfs, lbc, lbs, rc, rs, mc, mscl, ac, as_ = {}, {}, {}, {}, {}, {}, {}, {}, {}, {}
+        fw, bw, fs, apl, ag, rg, mpl, mg, ob = {}, {}, {}, {}, {}, {}, {}, {}, {}
+
+        def a1(b, t):
+            xs[b, t] = sb.tile([P, 4, P], F32, name=f"xs{b}{t}", tag="xs", bufs=3)
+            nc.vector.scalar_tensor_tensor(
+                out=xs[b, t][:],
+                in0=row_ps[b][:, 0:N].rearrange("p (c m) -> p c m", c=4),
+                scalar=wm1[:, t, b : b + 1],
+                in1=lk[b][:, t, :].rearrange("p (m c) -> p c m", c=4),
+                op0=ADD,
+                op1=MUL,
+            )
+
+        def a2(b, t):
+            if t == 0:
+                l2[b] = sb.tile([P, 4, N], F32, name=f"l2{b}", tag="l2", bufs=2)
+            nc.vector.scalar_tensor_tensor(
+                out=l2[b][:, t, :],
+                in0=row_ps[b][:, N : 2 * N],
+                scalar=sc[:, t, b : b + 1],
+                in1=xs[b, t][:].rearrange("p c m -> p (c m)"),
+                op0=MUL,
+                op1=SUB,
+            )
+
+        def tr(b, t):
+            tp[b, t] = ps.tile([P, 4, P], F32, name=f"tp{b}{t}", tag="tp", bufs=2)
+            for q in range(4):
+                nc.tensor.transpose(tp[b, t][:, q, :], l2[b][:, t, q * P : (q + 1) * P], ident[:])
+
+        def lf(b, t):
+            if t == 0:
+                lfg[b] = sb.tile([P, 4, P, 4], BF16, name=f"lfg{b}", tag="lfg", bufs=2, align_bytes=64)
+            nc.vector.tensor_tensor(
+                out=lfg[b][:, t, :, :],
+                in0=tp[b, t][:].rearrange("p q m -> p m q"),
+                in1=gm[:, t, :, :],
+                op=MUL,
+            )
+
+        def lb(b, t):
+            if b not in lbg:
+                lbg[b] = sb.tile([P, 4, P, 4], BF16, name=f"lbg{b}", tag="lbg", bufs=2, align_bytes=64)
+            eng = nc.vector if t in V_BLOCKS.get(b, ()) else nc.gpsimd
+            eng.tensor_tensor(
+                out=lbg[b][:, t, :, :],
+                in0=l2[b][:, :, t * P : (t + 1) * P].rearrange("p q m -> p m q"),
+                in1=gm[:, t, :, :],
+                op=MUL,
+            )
+
+        def codes(name, width, bufs=2):
+            c = sb.tile([P, width], U32, name=f"{name}_c", tag=f"{name[:-1]}_c", bufs=bufs, align_bytes=64)
+            s = sb.tile([P, width], U8, name=f"{name}_s", tag=f"{name[:-1]}_s", bufs=bufs, align_bytes=64)
+            return c, s
+
+        def quant(c, s, src, lo=0, hi=None):
+            hi = c.shape[1] if hi is None else hi
+            nc.vector.quantize_mx(out=c[:, lo:hi].bitcast(FP8X4), scales=s[:, lo:hi], in_=src[:, 4 * lo : 4 * hi])
+
+        def q_lf(b):
+            lfc[b], lfs[b] = codes(f"lf{b}", N)
+            quant(lfc[b], lfs[b], lfg[b][:].rearrange("p c m t -> p (c m t)"))
+
+        def q_lb(b, lo=0, hi=N):
+            if lo == 0:
+                lbc[b], lbs[b] = codes(f"lb{b}", N)
+            quant(lbc[b], lbs[b], lbg[b][:].rearrange("p c m t -> p (c m t)"), lo, hi)
+
+        def q_r(b):
+            rc[b], rs[b] = codes(f"r{b}", R)
+            quant(rc[b], rs[b], rg[b][:])
+
+        def q_m(b):
+            mc[b], mscl[b] = codes(f"m{b}", W, bufs=3)
+            quant(mc[b], mscl[b], mg[b][:])
+
+        def q_a(b, lo=0, hi=R):
+            if lo == 0:
+                ac[b], as_[b] = codes(f"a{b}", R)
+            quant(ac[b], as_[b], ag[b][:], lo, hi)
+
+        def r_turn(b):
+            bank = ps.tile([P, 2, 2, P], F32, name=f"rt{b}", tag="mm", bufs=4)
+            for a in range(2):
+                words = rr[b][:, a, :].bitcast(F32)
+                for u in range(2):
+                    nc.tensor.transpose(bank[:, a, u, :], words[:, u : N // 2 : 2], ident[:])
+            rg[b] = sb.tile([P, 4 * R], BF16, name=f"rg{b}", tag="rg", bufs=2, align_bytes=64)
+            nc.scalar.copy(
+                out=rg[b][:].bitcast(F32).rearrange("p (a n u) -> p a n u", a=2, u=2),
+                in_=bank[:].rearrange("p a u n -> p a n u"),
+            )
+
+        def m_widen(b):
+            mpl[b] = sb.tile([P, 4, W], BF16, name=f"mpl{b}", tag="mpl", bufs=2, align_bytes=64)
+            for t in range(4):
+                nc.scalar.activation(
+                    out=mpl[b][:, t, :], in_=mb[b][:, t, :].bitcast(FP8), func=COPY, scale=ms[:, t : t + 1]
+                )
+
+        def m_inter(b):
+            mg[b] = sb.tile([P, 4 * W], BF16, name=f"mg{b}", tag="mg", bufs=2, align_bytes=64)
+            dst = mg[b][:].rearrange("p (w t) -> p w t", t=4)
+            src = mpl[b][:].rearrange("p t w -> p w t")
+            for u in range(2):
+                s = slice(u * W // 2, (u + 1) * W // 2)
+                nc.scalar.copy(out=dst[:, s, :], in_=src[:, s, :])
+
+        def product(b, dct, c, s, halves=(0, 1)):
+            for u in halves:
+                dct[b, u] = ps.tile([P, 2, R], F32, name=f"pr{b}{u}", tag="mm", bufs=4)
+                for v in range(2):
+                    cols = slice((2 * u + v) * P, (2 * u + v + 1) * P)
+                    nc.tensor.matmul_mx(
+                        out=dct[b, u][:, v, :],
+                        lhsT=c[:, cols].bitcast(FP8X4),
+                        lhsT_scale=s[:, cols],
+                        rhs=rc[b][:].bitcast(FP8X4),
+                        rhs_scale=rs[b][:],
+                        start=True,
+                        stop=True,
+                    )
+
+        def fs_copy(b):
+            fs[b] = sb.tile([P, 4, R], F32, name=f"fs{b}", tag="fs", bufs=2)
+            for t in range(4):
+                nc.scalar.activation(
+                    out=fs[b][:, t, :], in_=fw[b, t // 2][:, t % 2, :], func=COPY, scale=h7[:, t : t + 1]
+                )
+
+        def mix(b, t):
+            if t == 0:
+                apl[b] = sb.tile([P, 4, R], BF16, name=f"apl{b}", tag="apl", bufs=2)
+            nc.vector.scalar_tensor_tensor(
+                out=apl[b][:, t, :],
+                in0=bw[b, t // 2][:, t % 2, :],
+                scalar=h3[:, t : t + 1],
+                in1=fs[b][:, t, :],
+                op0=MUL,
+                op1=ADD,
+            )
+
+        def a_inter(b, half, on_vector=False):
+            if half == 0:
+                ag[b] = sb.tile([P, 4 * R], BF16, name=f"ag{b}", tag="ag", bufs=2, align_bytes=64)
+            s = slice(half * P, (half + 1) * P)
+            dst = ag[b][:].rearrange("p (k t) -> p k t", t=4)[:, s, :]
+            src = apl[b][:].rearrange("p t k -> p k t")[:, s, :]
+            if on_vector:
+                nc.vector.tensor_copy(out=dst, in_=src)
+            else:
+                nc.scalar.copy(out=dst, in_=src)
+
+        def readout(b, a):
+            bank = ps.tile([P, W], F32, name=f"ro{b}{a}", tag="mm", bufs=4)
+            nc.tensor.matmul_mx(
+                out=bank[:],
+                lhsT=ac[b][:, a * P : (a + 1) * P].bitcast(FP8X4),
+                lhsT_scale=as_[b][:, a * P : (a + 1) * P],
+                rhs=mc[b][:].bitcast(FP8X4),
+                rhs_scale=mscl[b][:],
+                start=True,
+                stop=True,
+            )
+            return bank
+
+        def out_copy(b, a, bank, on_vector=False):
+            if a == 0:
+                ob[b] = sb.tile([P, 2, W], F32, name=f"ob{b}", tag="ob", bufs=2)
+            if on_vector:
+                nc.vector.tensor_copy(out=ob[b][:, a, :], in_=bank[:])
+            else:
+                nc.scalar.copy(out=ob[b][:, a, :], in_=bank[:])
+
+        def store(b, a0=0, a1_=2):
+            nc.sync.dma_start(
+                out=out[b].rearrange("(p a) w -> p a w", a=2)[:, a0:a1_, :], in_=ob[b][:, a0:a1_, :]
+            )
+
+        def finish(b):
+            q_a(b)
+            banks = [readout(b, a) for a in range(2)]
+            for a in range(2):
+                out_copy(b, a, banks[a])
+            store(b)
+
+        for b in range(B):
+            a1(b, 0)
+            a1(b, 1)
+            if b >= 1:
+                fs_copy(b - 1)
+            a2(b, 0)
+            tr(b, 0)
+            if b >= 2:
+                finish(b - 2)
+            a1(b, 2)
+            a2(b, 1)
+            tr(b, 1)
+            lf(b, 0)
+            a1(b, 3)
+            if b == 1:
+                m_inter(1)
+                q_m(0)
+            if b == 2:
+                m_widen(3)
+                q_m(2)
+            if b == 3:
+                q_m(3)
+            a2(b, 2)
+            tr(b, 2)
+            r_turn(b)
+            lf(b, 1)
+            if b >= 1:
+                q_lb(b - 1)
+                product(b - 1, bw, lbc[b - 1], lbs[b - 1])
+            a2(b, 3)
+            tr(b, 3)
+            for t in range(4):
+                if t not in V_BLOCKS.get(b, ()):
+                    lb(b, t)
+            if b == 0:
+                m_widen(0)
+                m_inter(0)
+                m_widen(1)
+            if b == 1:
+                m_widen(2)
+            lf(b, 2)
+            if b + 1 < B:
+                broadcast_rows(b + 1)
+            q_r(b)
+            lf(b, 3)
+            if b >= 1:
+                for t in range(4):
+                    mix(b - 1, t)
+                a_inter(b - 1, 0)
+                a_inter(b - 1, 1)
+            if b == 1:
+                m_inter(2)
+                q_m(1)
+            if b == 2:
+                m_inter(3)
+            for t in V_BLOCKS.get(b, ()):
+                lb(b, t)
+            q_lf(b)
+            product(b, fw, lfc[b], lfs[b])
+
+        last = B - 1
+        q_lb(last, 0, N // 2)
+        product(last, bw, lbc[last], lbs[last], (0,))
+        fs_copy(last)
+        q_lb(last, N // 2, N)
+        product(last, bw, lbc[last], lbs[last], (1,))
+        finish(last - 1)
+        for t in range(4):
+            mix(last, t)
+        a_inter(last, 0)
+        a_inter(last, 1, on_vector=True)
+        banks = []
+        for a in (1, 0):
+            if a == 1:
+                ac[last], as_[last] = codes(f"a{last}", R)
+            quant(ac[last], as_[last], ag[last][:], a * P, (a + 1) * P)
+            banks.append(readout(last, a))
+        out_copy(last, 0, banks[1])
+        out_copy(last, 1, banks[0], on_vector=True)
+        store(last, 1, 2)
+        store(last, 0, 1)

@@ -18,7 +18,7 @@ MUL = mybir.AluOpType.mult
 COPY = mybir.ActivationFunctionType.Copy
 
 P = 128
-V_BLOCKS = {3: (0, 1)}
+V_BLOCKS = {3: (0, 1, 2)}
 
 
 def tile_dnctemporallinkreadout_kernel(tc, link, w, p, r, g, h, m_bytes, m_scale, out):
@@ -30,14 +30,16 @@ def tile_dnctemporallinkreadout_kernel(tc, link, w, p, r, g, h, m_bytes, m_scale
 
         rows = sb.tile([P, N], BF16, name="rows")
         nc.vector.memset(rows[:], 0.0)
+        rows_gh = sb.tile([P, N], BF16, name="rows_gh")
+        nc.vector.memset(rows_gh[:], 0.0)
         ident_bf = sb.tile([P, P], BF16, name="ident_bf")
         make_identity(nc, ident_bf[:])
         ident = sb.tile([P, P], F32, name="ident")
         make_identity(nc, ident[:])
-        nc.scalar.dma_start(out=rows[0:4, :], in_=w)
-        nc.scalar.dma_start(out=rows[4:8, :], in_=p)
-        nc.scalar.dma_start(out=rows[8:9, :], in_=g.rearrange("(o n) -> o n", o=1))
-        nc.scalar.dma_start(out=rows[9:10, :], in_=h.rearrange("(o n) -> o n", o=1))
+        nc.sync.dma_start(out=rows[0:4, :], in_=w)
+        nc.sync.dma_start(out=rows[4:8, :], in_=p)
+        nc.scalar.dma_start(out=rows_gh[0:1, :], in_=g.rearrange("(o n) -> o n", o=1))
+        nc.scalar.dma_start(out=rows_gh[1:2, :], in_=h.rearrange("(o n) -> o n", o=1))
         ms = sb.tile([P, 4], F32, name="ms")
         nc.scalar.dma_start(out=ms[:], in_=m_scale.rearrange("o (p t) x -> p (o t x)", t=4))
 
@@ -93,16 +95,19 @@ def tile_dnctemporallinkreadout_kernel(tc, link, w, p, r, g, h, m_bytes, m_scale
                 )
 
         broadcast_rows(0)
-        sc = sb.tile([P, 4, 10], F32, name="sc")
-        nc.vector.tensor_copy(out=sc[:], in_=scp[:, :, 0:10])
+        sc = sb.tile([P, 4, 4], F32, name="sc")
+        nc.vector.tensor_copy(out=sc[:], in_=scp[:, :, 0:4])
         wm1 = sb.tile([P, 4, 4], F32, name="wm1")
-        nc.vector.tensor_scalar(out=wm1[:], in0=sc[:, :, 0:4], scalar1=-1.0, scalar2=None, op0=ADD)
+        nc.vector.tensor_scalar(out=wm1[:], in0=scp[:, :, 0:4], scalar1=-1.0, scalar2=None, op0=ADD)
+        ghp = ps.tile([P, 4, P], BF16, name="ghp", tag="tp", bufs=2)
+        for t in range(4):
+            nc.tensor.transpose(ghp[:, t, :], rows_gh[:, t : N : 4], ident_bf[:])
         g4 = sb.tile([P, 4], F32, name="g4")
-        nc.scalar.copy(out=g4[:], in_=sc[:, :, 8])
+        nc.scalar.copy(out=g4[:], in_=ghp[:, :, 0])
         h7 = sb.tile([P, 4], F32, name="h7")
-        nc.scalar.activation(out=h7[:], in_=sc[:, :, 9], func=COPY, scale=0.7)
+        nc.scalar.activation(out=h7[:], in_=ghp[:, :, 1], func=COPY, scale=0.7)
         h3 = sb.tile([P, 4], F32, name="h3")
-        nc.scalar.activation(out=h3[:], in_=sc[:, :, 9], func=COPY, scale=0.3)
+        nc.scalar.activation(out=h3[:], in_=ghp[:, :, 1], func=COPY, scale=0.3)
         gm = sb.tile([P, 4, P, 4], BF16, name="gm", align_bytes=64)
         for t in range(4):
             nc.scalar.copy(out=gm[:, t, :, :], in_=g4[:].unsqueeze(1).to_broadcast([P, P, 4]))
@@ -152,7 +157,7 @@ def tile_dnctemporallinkreadout_kernel(tc, link, w, p, r, g, h, m_bytes, m_scale
 
         def lb(b, t):
             if b not in lbg:
-                lbg[b] = sb.tile([P, 4, P, 4], BF16, name=f"lbg{b}", tag="lbg", bufs=2, align_bytes=64)
+                lbg[b] = sb.tile([P, 4, P, 4], BF16, name=f"lbg{b}", tag="lbg" if b < B - 1 else "lbg_last", bufs=1, align_bytes=64)
             eng = nc.vector if t in V_BLOCKS.get(b, ()) else nc.gpsimd
             eng.tensor_tensor(
                 out=lbg[b][:, t, :, :],
@@ -180,7 +185,7 @@ def tile_dnctemporallinkreadout_kernel(tc, link, w, p, r, g, h, m_bytes, m_scale
             quant(lbc[b], lbs[b], lbg[b][:].rearrange("p c m t -> p (c m t)"), lo, hi)
 
         def q_r(b):
-            rc[b], rs[b] = codes(f"r{b}", R)
+            rc[b], rs[b] = codes(f"r{b}", R, bufs=3)
             quant(rc[b], rs[b], rg[b][:])
 
         def q_m(b):
@@ -290,91 +295,110 @@ def tile_dnctemporallinkreadout_kernel(tc, link, w, p, r, g, h, m_bytes, m_scale
                 out=out[b].rearrange("(p a) w -> p a w", a=2)[:, a0:a1_, :], in_=ob[b][:, a0:a1_, :]
             )
 
-        def finish(b):
-            q_a(b)
+        def read_out(b):
             banks = [readout(b, a) for a in range(2)]
             for a in range(2):
                 out_copy(b, a, banks[a])
             store(b)
 
         for b in range(B):
+            last = b == B - 1
+            if b >= 2:
+                product(b - 2, bw, lbc[b - 2], lbs[b - 2])
             a1(b, 0)
             a1(b, 1)
             if b >= 1:
                 fs_copy(b - 1)
+            if b >= 3:
+                read_out(b - 3)
             a2(b, 0)
             tr(b, 0)
             if b >= 2:
-                finish(b - 2)
+                mix(b - 2, 0)
             a1(b, 2)
+            if b >= 2:
+                mix(b - 2, 1)
             a2(b, 1)
             tr(b, 1)
+            r_turn(b)
             lf(b, 0)
+            if b >= 2:
+                mix(b - 2, 2)
             a1(b, 3)
-            if b == 1:
-                m_inter(1)
-                q_m(0)
-            if b == 2:
-                m_widen(3)
-                q_m(2)
-            if b == 3:
-                q_m(3)
+            if b >= 2:
+                mix(b - 2, 3)
             a2(b, 2)
             tr(b, 2)
-            r_turn(b)
-            lf(b, 1)
-            if b >= 1:
-                q_lb(b - 1)
-                product(b - 1, bw, lbc[b - 1], lbs[b - 1])
-            a2(b, 3)
-            tr(b, 3)
-            for t in range(4):
-                if t not in V_BLOCKS.get(b, ()):
-                    lb(b, t)
+            if b == 1:
+                m_inter(1)
+            if b == 2:
+                m_inter(2)
+            if b >= 2:
+                a_inter(b - 2, 0)
+                a_inter(b - 2, 1)
             if b == 0:
                 m_widen(0)
                 m_inter(0)
                 m_widen(1)
-            if b == 1:
-                m_widen(2)
+            elif b < 3:
+                m_widen(b + 1)
+            else:
+                m_inter(3)
+            lf(b, 1)
+            a2(b, 3)
+            tr(b, 3)
             lf(b, 2)
             if b + 1 < B:
                 broadcast_rows(b + 1)
             q_r(b)
-            lf(b, 3)
             if b >= 1:
+                q_m(b - 1)
+            lf(b, 3)
+            if b >= 2:
+                q_a(b - 2)
+            if last:
+                q_lb(b - 1)
+                product(b - 1, bw, lbc[b - 1], lbs[b - 1])
+                read_out(b - 2)
                 for t in range(4):
-                    mix(b - 1, t)
-                a_inter(b - 1, 0)
-                a_inter(b - 1, 1)
-            if b == 1:
-                m_inter(2)
-                q_m(1)
-            if b == 2:
-                m_inter(3)
-            for t in V_BLOCKS.get(b, ()):
-                lb(b, t)
-            q_lf(b)
-            product(b, fw, lfc[b], lfs[b])
+                    lb(b, t)
+                    if t == 1:
+                        q_lf(b)
+                        product(b, fw, lfc[b], lfs[b])
+                    if t == 2:
+                        q_lb(b, 0, N // 2)
+                        product(b, bw, lbc[b], lbs[b], (0,))
+            else:
+                q_lf(b)
+                product(b, fw, lfc[b], lfs[b])
+                if b >= 1:
+                    q_lb(b - 1)
+                for t in range(4):
+                    lb(b, t)
 
-        last = B - 1
-        q_lb(last, 0, N // 2)
-        product(last, bw, lbc[last], lbs[last], (0,))
-        fs_copy(last)
-        q_lb(last, N // 2, N)
-        product(last, bw, lbc[last], lbs[last], (1,))
-        finish(last - 1)
+        z = B - 1
         for t in range(4):
-            mix(last, t)
-        a_inter(last, 0)
-        a_inter(last, 1, on_vector=True)
-        banks = []
+            mix(z - 1, t)
+        fs_copy(z)
+        q_lb(z, N // 2, N)
+        product(z, bw, lbc[z], lbs[z], (1,))
+        a_inter(z - 1, 0)
+        a_inter(z - 1, 1, on_vector=True)
+        q_m(z)
+        mix(z, 0)
+        q_a(z - 1)
+        read_out(z - 1)
+        for t in range(1, 4):
+            mix(z, t)
+        a_inter(z, 0)
+        a_inter(z, 1, on_vector=True)
+        banks = {}
         for a in (1, 0):
             if a == 1:
-                ac[last], as_[last] = codes(f"a{last}", R)
-            quant(ac[last], as_[last], ag[last][:], a * P, (a + 1) * P)
-            banks.append(readout(last, a))
-        out_copy(last, 0, banks[1])
-        out_copy(last, 1, banks[0], on_vector=True)
-        store(last, 1, 2)
-        store(last, 0, 1)
+                ac[z], as_[z] = codes(f"a{z}", R)
+            quant(ac[z], as_[z], ag[z][:], a * P, (a + 1) * P)
+            banks[a] = readout(z, a)
+        out_copy(z, 0, banks[0])
+        out_copy(z, 1, banks[1], on_vector=True)
+        store(z, 1, 2)
+        store(z, 0, 1)

from contextlib import ExitStack

import concourse.mybir as mybir
from concourse.masks import make_identity

B, N, R, W = 4, 512, 256, 512
FLOPS = 3 * B * 2 * R * N * N

F32 = mybir.dt.float32
BF16 = mybir.dt.bfloat16
U32 = mybir.dt.uint32
U8 = mybir.dt.uint8
FP8 = mybir.dt.float8_e4m3fn
FP8X4 = mybir.dt.float8_e4m3fn_x4
ADD = mybir.AluOpType.add
SUB = mybir.AluOpType.subtract
MUL = mybir.AluOpType.mult
COPY = mybir.ActivationFunctionType.Copy

P = 128
V_BLOCKS = {3: (0, 1, 2)}


def tile_dnctemporallinkreadout_kernel(tc, link, w, p, r, g, h, m_bytes, m_scale, out):
    nc = tc.nc
    with ExitStack() as ctx:
        sb = ctx.enter_context(tc.tile_pool(name="sb", bufs=1))
        ps = ctx.enter_context(tc.psum_pool(name="ps", bufs=1))
        ctx.enter_context(tc.manual_schedule())

        rows = sb.tile([P, N], BF16, name="rows")
        nc.vector.memset(rows[:], 0.0)
        rows_gh = sb.tile([P, N], BF16, name="rows_gh")
        nc.vector.memset(rows_gh[:], 0.0)
        ident_bf = sb.tile([P, P], BF16, name="ident_bf")
        make_identity(nc, ident_bf[:])
        ident = sb.tile([P, P], F32, name="ident")
        make_identity(nc, ident[:])
        nc.sync.dma_start(out=rows[0:4, :], in_=w)
        nc.sync.dma_start(out=rows[4:8, :], in_=p)
        nc.scalar.dma_start(out=rows_gh[0:1, :], in_=g.rearrange("(o n) -> o n", o=1))
        nc.scalar.dma_start(out=rows_gh[1:2, :], in_=h.rearrange("(o n) -> o n", o=1))
        ms = sb.tile([P, 4], F32, name="ms")
        nc.scalar.dma_start(out=ms[:], in_=m_scale.rearrange("o (p t) x -> p (o t x)", t=4))

        lk = {}
        rr = {}
        mb = {}

        def load_link(b):
            lk[b] = sb.tile([P, 4, N], BF16, name=f"lk{b}", align_bytes=64)
            src = link[b].rearrange("(p t) j -> p t j", t=4)
            for u in range(2):
                nc.sync.dma_start(out=lk[b][:, 2 * u : 2 * u + 2, :], in_=src[:, 2 * u : 2 * u + 2, :])

        def load_r(b):
            rr[b] = sb.tile([P, 2, N], BF16, name=f"rr{b}", align_bytes=64)
            nc.sync.dma_start(out=rr[b][:], in_=r[b].rearrange("(p a) j -> p a j", a=2))

        def load_m(b):
            mb[b] = sb.tile([P, 4, W], U8, name=f"mb{b}", align_bytes=64)
            nc.sync.dma_start(out=mb[b][:], in_=m_bytes[b].rearrange("(p t) w -> p t w", t=4))

        load_link(0)
        load_r(0)
        load_m(0)
        load_link(1)
        load_m(1)
        load_r(1)
        load_link(2)
        load_m(2)
        load_r(2)
        load_link(3)
        load_m(3)
        load_r(3)

        not_i = sb.tile([P, P], F32, name="not_i")
        nc.vector.tensor_scalar(out=not_i[:], in0=ident[:], scalar1=-1.0, scalar2=1.0, op0=MUL, op1=ADD)
        scp = ps.tile([P, 4, P], BF16, name="scp", tag="tp", bufs=2)
        for t in range(4):
            nc.tensor.transpose(scp[:, t, :], rows[:, t : N : 4], ident_bf[:])

        row_ps = {}

        def broadcast_rows(b):
            row_ps[b] = ps.tile([P, 2 * N], BF16, name=f"row_ps{b}", tag="row", bufs=2)
            for u in range(2):
                k = 4 * u + b
                nc.tensor.matmul(
                    row_ps[b][:, u * N : (u + 1) * N].rearrange("p (t m) -> p t m", t=4),
                    lhsT=ident_bf[:, k : k + 1].to_broadcast([P, P]),
                    rhs=rows[:].rearrange("k (m t) -> k t m", t=4),
                    start=True,
                    stop=True,
                )

        broadcast_rows(0)
        sc = sb.tile([P, 4, 4], F32, name="sc")
        nc.vector.tensor_copy(out=sc[:], in_=scp[:, :, 0:4])
        wm1 = sb.tile([P, 4, 4], F32, name="wm1")
        nc.vector.tensor_scalar(out=wm1[:], in0=scp[:, :, 0:4], scalar1=-1.0, scalar2=None, op0=ADD)
        ghp = ps.tile([P, 4, P], BF16, name="ghp", tag="tp", bufs=2)
        for t in range(4):
            nc.tensor.transpose(ghp[:, t, :], rows_gh[:, t : N : 4], ident_bf[:])
        g4 = sb.tile([P, 4], F32, name="g4")
        nc.scalar.copy(out=g4[:], in_=ghp[:, :, 0])
        h7 = sb.tile([P, 4], F32, name="h7")
        nc.scalar.activation(out=h7[:], in_=ghp[:, :, 1], func=COPY, scale=0.7)
        h3 = sb.tile([P, 4], F32, name="h3")
        nc.scalar.activation(out=h3[:], in_=ghp[:, :, 1], func=COPY, scale=0.3)
        gm = sb.tile([P, 4, P, 4], BF16, name="gm", align_bytes=64)
        for t in range(4):
            nc.scalar.copy(out=gm[:, t, :, :], in_=g4[:].unsqueeze(1).to_broadcast([P, P, 4]))
            nc.scalar.activation(out=gm[:, t, :, t], in_=not_i[:], func=COPY, scale=g4[:, t : t + 1])

        xs, l2, tp, lfg, lbg = {}, {}, {}, {}, {}
        lfc, lfs, lbc, lbs, rc, rs, mc, mscl, ac, as_ = {}, {}, {}, {}, {}, {}, {}, {}, {}, {}
        fw, bw, fs, apl, ag, rg, mpl, mg, ob = {}, {}, {}, {}, {}, {}, {}, {}, {}

        def a1(b, t):
            xs[b, t] = sb.tile([P, 4, P], F32, name=f"xs{b}{t}", tag="xs", bufs=3)
            nc.vector.scalar_tensor_tensor(
                out=xs[b, t][:],
                in0=row_ps[b][:, 0:N].rearrange("p (c m) -> p c m", c=4),
                scalar=wm1[:, t, b : b + 1],
                in1=lk[b][:, t, :].rearrange("p (m c) -> p c m", c=4),
                op0=ADD,
                op1=MUL,
            )

        def a2(b, t):
            if t == 0:
                l2[b] = sb.tile([P, 4, N], F32, name=f"l2{b}", tag="l2", bufs=2)
            nc.vector.scalar_tensor_tensor(
                out=l2[b][:, t, :],
                in0=row_ps[b][:, N : 2 * N],
                scalar=sc[:, t, b : b + 1],
                in1=xs[b, t][:].rearrange("p c m -> p (c m)"),
                op0=MUL,
                op1=SUB,
            )

        def tr(b, t):
            tp[b, t] = ps.tile([P, 4, P], F32, name=f"tp{b}{t}", tag="tp", bufs=2)
            for q in range(4):
                nc.tensor.transpose(tp[b, t][:, q, :], l2[b][:, t, q * P : (q + 1) * P], ident[:])

        def lf(b, t):
            if t == 0:
                lfg[b] = sb.tile([P, 4, P, 4], BF16, name=f"lfg{b}", tag="lfg", bufs=2, align_bytes=64)
            nc.vector.tensor_tensor(
                out=lfg[b][:, t, :, :],
                in0=tp[b, t][:].rearrange("p q m -> p m q"),
                in1=gm[:, t, :, :],
                op=MUL,
            )

        def lb(b, t):
            if b not in lbg:
                lbg[b] = sb.tile([P, 4, P, 4], BF16, name=f"lbg{b}", tag="lbg" if b < B - 1 else "lbg_last", bufs=1, align_bytes=64)
            eng = nc.vector if t in V_BLOCKS.get(b, ()) else nc.gpsimd
            eng.tensor_tensor(
                out=lbg[b][:, t, :, :],
                in0=l2[b][:, :, t * P : (t + 1) * P].rearrange("p q m -> p m q"),
                in1=gm[:, t, :, :],
                op=MUL,
            )

        def codes(name, width, bufs=2):
            c = sb.tile([P, width], U32, name=f"{name}_c", tag=f"{name[:-1]}_c", bufs=bufs, align_bytes=64)
            s = sb.tile([P, width], U8, name=f"{name}_s", tag=f"{name[:-1]}_s", bufs=bufs, align_bytes=64)
            return c, s

        def quant(c, s, src, lo=0, hi=None):
            hi = c.shape[1] if hi is None else hi
            nc.vector.quantize_mx(out=c[:, lo:hi].bitcast(FP8X4), scales=s[:, lo:hi], in_=src[:, 4 * lo : 4 * hi])

        def q_lf(b):
            lfc[b], lfs[b] = codes(f"lf{b}", N)
            quant(lfc[b], lfs[b], lfg[b][:].rearrange("p c m t -> p (c m t)"))

        def q_lb(b, lo=0, hi=N):
            if lo == 0:
                lbc[b], lbs[b] = codes(f"lb{b}", N)
            quant(lbc[b], lbs[b], lbg[b][:].rearrange("p c m t -> p (c m t)"), lo, hi)

        def q_r(b):
            rc[b], rs[b] = codes(f"r{b}", R, bufs=3)
            quant(rc[b], rs[b], rg[b][:])

        def q_m(b):
            mc[b], mscl[b] = codes(f"m{b}", W, bufs=3)
            quant(mc[b], mscl[b], mg[b][:])

        def q_a(b, lo=0, hi=R):
            if lo == 0:
                ac[b], as_[b] = codes(f"a{b}", R)
            quant(ac[b], as_[b], ag[b][:], lo, hi)

        def r_turn(b):
            bank = ps.tile([P, 2, 2, P], F32, name=f"rt{b}", tag="mm", bufs=4)
            for a in range(2):
                words = rr[b][:, a, :].bitcast(F32)
                for u in range(2):
                    nc.tensor.transpose(bank[:, a, u, :], words[:, u : N // 2 : 2], ident[:])
            rg[b] = sb.tile([P, 4 * R], BF16, name=f"rg{b}", tag="rg", bufs=2, align_bytes=64)
            nc.scalar.copy(
                out=rg[b][:].bitcast(F32).rearrange("p (a n u) -> p a n u", a=2, u=2),
                in_=bank[:].rearrange("p a u n -> p a n u"),
            )

        def m_widen(b):
            mpl[b] = sb.tile([P, 4, W], BF16, name=f"mpl{b}", tag="mpl", bufs=2, align_bytes=64)
            for t in range(4):
                nc.scalar.activation(
                    out=mpl[b][:, t, :], in_=mb[b][:, t, :].bitcast(FP8), func=COPY, scale=ms[:, t : t + 1]
                )

        def m_inter(b):
            mg[b] = sb.tile([P, 4 * W], BF16, name=f"mg{b}", tag="mg", bufs=2, align_bytes=64)
            dst = mg[b][:].rearrange("p (w t) -> p w t", t=4)
            src = mpl[b][:].rearrange("p t w -> p w t")
            for u in range(2):
                s = slice(u * W // 2, (u + 1) * W // 2)
                nc.scalar.copy(out=dst[:, s, :], in_=src[:, s, :])

        def product(b, dct, c, s, halves=(0, 1)):
            for u in halves:
                dct[b, u] = ps.tile([P, 2, R], F32, name=f"pr{b}{u}", tag="mm", bufs=4)
                for v in range(2):
                    cols = slice((2 * u + v) * P, (2 * u + v + 1) * P)
                    nc.tensor.matmul_mx(
                        out=dct[b, u][:, v, :],
                        lhsT=c[:, cols].bitcast(FP8X4),
                        lhsT_scale=s[:, cols],
                        rhs=rc[b][:].bitcast(FP8X4),
                        rhs_scale=rs[b][:],
                        start=True,
                        stop=True,
                    )

        def fs_copy(b):
            fs[b] = sb.tile([P, 4, R], F32, name=f"fs{b}", tag="fs", bufs=2)
            for t in range(4):
                nc.scalar.activation(
                    out=fs[b][:, t, :], in_=fw[b, t // 2][:, t % 2, :], func=COPY, scale=h7[:, t : t + 1]
                )

        def mix(b, t):
            if t == 0:
                apl[b] = sb.tile([P, 4, R], BF16, name=f"apl{b}", tag="apl", bufs=2)
            nc.vector.scalar_tensor_tensor(
                out=apl[b][:, t, :],
                in0=bw[b, t // 2][:, t % 2, :],
                scalar=h3[:, t : t + 1],
                in1=fs[b][:, t, :],
                op0=MUL,
                op1=ADD,
            )

        def a_inter(b, half, on_vector=False):
            if half == 0:
                ag[b] = sb.tile([P, 4 * R], BF16, name=f"ag{b}", tag="ag", bufs=2, align_bytes=64)
            s = slice(half * P, (half + 1) * P)
            dst = ag[b][:].rearrange("p (k t) -> p k t", t=4)[:, s, :]
            src = apl[b][:].rearrange("p t k -> p k t")[:, s, :]
            if on_vector:
                nc.vector.tensor_copy(out=dst, in_=src)
            else:
                nc.scalar.copy(out=dst, in_=src)

        def readout(b, a):
            bank = ps.tile([P, W], F32, name=f"ro{b}{a}", tag="mm", bufs=4)
            nc.tensor.matmul_mx(
                out=bank[:],
                lhsT=ac[b][:, a * P : (a + 1) * P].bitcast(FP8X4),
                lhsT_scale=as_[b][:, a * P : (a + 1) * P],
                rhs=mc[b][:].bitcast(FP8X4),
                rhs_scale=mscl[b][:],
                start=True,
                stop=True,
            )
            return bank

        def out_copy(b, a, bank, on_vector=False):
            if a == 0:
                ob[b] = sb.tile([P, 2, W], F32, name=f"ob{b}", tag="ob", bufs=2)
            if on_vector:
                nc.vector.tensor_copy(out=ob[b][:, a, :], in_=bank[:])
            else:
                nc.scalar.copy(out=ob[b][:, a, :], in_=bank[:])

        def store(b, a0=0, a1_=2):
            nc.sync.dma_start(
                out=out[b].rearrange("(p a) w -> p a w", a=2)[:, a0:a1_, :], in_=ob[b][:, a0:a1_, :]
            )

        def read_out(b):
            banks = [readout(b, a) for a in range(2)]
            for a in range(2):
                out_copy(b, a, banks[a])
            store(b)

        for b in range(B):
            last = b == B - 1
            if b >= 2:
                product(b - 2, bw, lbc[b - 2], lbs[b - 2])
            a1(b, 0)
            a1(b, 1)
            if b >= 1:
                fs_copy(b - 1)
            if b >= 3:
                read_out(b - 3)
            a2(b, 0)
            tr(b, 0)
            if b >= 2:
                mix(b - 2, 0)
            a1(b, 2)
            if b >= 2:
                mix(b - 2, 1)
            a2(b, 1)
            tr(b, 1)
            r_turn(b)
            lf(b, 0)
            if b >= 2:
                mix(b - 2, 2)
            a1(b, 3)
            if b >= 2:
                mix(b - 2, 3)
            a2(b, 2)
            tr(b, 2)
            if b == 1:
                m_inter(1)
            if b == 2:
                m_inter(2)
            if b >= 2:
                a_inter(b - 2, 0)
                a_inter(b - 2, 1)
            if b == 0:
                m_widen(0)
                m_inter(0)
                m_widen(1)
            elif b < 3:
                m_widen(b + 1)
            else:
                m_inter(3)
            lf(b, 1)
            a2(b, 3)
            tr(b, 3)
            lf(b, 2)
            if b + 1 < B:
                broadcast_rows(b + 1)
            q_r(b)
            if b >= 1:
                q_m(b - 1)
            lf(b, 3)
            if b >= 2:
                q_a(b - 2)
            if last:
                q_lb(b - 1)
                product(b - 1, bw, lbc[b - 1], lbs[b - 1])
                read_out(b - 2)
                for t in range(4):
                    lb(b, t)
                    if t == 1:
                        q_lf(b)
                        product(b, fw, lfc[b], lfs[b])
                    if t == 2:
                        q_lb(b, 0, N // 2)
                        product(b, bw, lbc[b], lbs[b], (0,))
            else:
                q_lf(b)
                product(b, fw, lfc[b], lfs[b])
                if b >= 1:
                    q_lb(b - 1)
                for t in range(4):
                    lb(b, t)

        z = B - 1
        for t in range(4):
            mix(z - 1, t)
        fs_copy(z)
        q_lb(z, N // 2, N)
        product(z, bw, lbc[z], lbs[z], (1,))
        a_inter(z - 1, 0)
        a_inter(z - 1, 1, on_vector=True)
        q_m(z)
        mix(z, 0)
        q_a(z - 1)
        read_out(z - 1)
        for t in range(1, 4):
            mix(z, t)
        a_inter(z, 0)
        a_inter(z, 1, on_vector=True)
        banks = {}
        for a in (1, 0):
            if a == 1:
                ac[z], as_[z] = codes(f"a{z}", R)
            quant(ac[z], as_[z], ag[z][:], a * P, (a + 1) * P)
            banks[a] = readout(z, a)
        out_copy(z, 0, banks[0])
        out_copy(z, 1, banks[1], on_vector=True)
        store(z, 1, 2)
        store(z, 0, 1)
